import numpy as np
import ml_dtypes


def mxq(x, axis, fmt="e4m3"):
    dtype, down = {"e4m3": (ml_dtypes.float8_e4m3fn, 7), "e5m2": (ml_dtypes.float8_e5m2, 14)}[fmt]
    v = np.moveaxis(np.asarray(x, np.float32).astype(ml_dtypes.bfloat16).astype(np.float64), axis, -1)
    blocks = v.reshape(v.shape[:-1] + (-1, 32))
    amax = np.abs(blocks).max(-1, keepdims=True)
    byte = np.maximum(np.where(amax > 0, np.frexp(amax)[1] - 1 + 127, 0) - down, 1)
    scale = np.exp2(byte - 127.0)
    codes = (blocks / scale).astype(np.float32).astype(dtype).astype(np.float64)
    return np.moveaxis((codes * scale).reshape(v.shape), -1, axis)


WIDE = False


def mx_kscale(k):
    if not WIDE:
        return np.ones(k)
    levels = np.array([10, -10, 5, -5, 0])
    if k % 512:
        return np.exp2(np.random.permutation(np.resize(levels, k // 32))).repeat(32)
    a = np.empty((k // 512, 16))
    for p in range(k // 512):
        a[p, :8] = np.random.permutation(np.resize(levels, 8))
        for g in range(8):
            far = levels[np.abs(levels - a[p, g]) >= 10]
            a[p, g + 8] = far[np.random.randint(len(far))]
    return np.exp2(a.ravel()).repeat(32)


def f64(x):
    return np.asarray(x).astype(np.float64)


def striped(idx):
    return np.tile(idx.reshape(-1, 16).T, (8, 1)).astype(np.uint16)


def unstriped(offs):
    return offs[:16].T.reshape(-1).astype(np.int64)


def pack_weight(w):
    k, n = w.shape
    w = f64(np.asarray(w, np.float32).astype(ml_dtypes.bfloat16)).reshape(k // 32, 32, n)
    amax = np.abs(w).max(1)
    byte = np.clip(np.where(amax > 0, np.frexp(amax)[1] - 1 + 127 - 7, 1), 1, 254)
    scaled = (w * np.exp2(127.0 - byte)[:, None, :]).reshape(k, n).astype(np.float32)
    words = np.ascontiguousarray(scaled.reshape(k // 512, 128, 4, n).transpose(0, 1, 3, 2)).astype(ml_dtypes.float8_e4m3fn).view(np.uint8)
    return words, np.ascontiguousarray(byte.astype(np.uint8).reshape(k // 512, 16, n))


def unpack_weight(words, scales):
    g, p, n, _ = words.shape
    vals = np.ascontiguousarray(words).view(ml_dtypes.float8_e4m3fn).astype(np.float64) * np.repeat(np.exp2(scales.astype(np.float64) - 127.0), 8, axis=1)[..., None]
    return vals.transpose(0, 1, 3, 2).reshape(g * 512, n)


def silu(v):
    return v / (1.0 + np.exp(-np.maximum(v, -700.0)))


K, T, S, V, H, N, J = 1024, 2048, 1024, 512, 512, 128, 512


def setup_inputs():
    n = np.random.standard_normal
    s = mx_kscale(K)[:, None]
    u = mx_kscale(H)
    r = mx_kscale(J)[:, None]
    packed_xT = pack_weight(n((K, T)) * s)
    return {
        "x_words": packed_xT[0],
        "x_scales": packed_xT[1],
        "eT": (n((J, V)) * r).astype(np.float32),
        "w1": (n((K, H)) / np.sqrt(3 * K) / s * u).astype(np.float32),
        "w2": (n((K, H)) / np.sqrt(3 * K) / s * u).astype(np.float32),
        "w3": (n((J, H)) / np.sqrt(3 * J) / r * u).astype(np.float32),
        "w4": (n((H, N)) / np.sqrt(H) / u[:, None]).astype(np.float32),
        "offs": striped(np.random.permutation(T)[:S]),
    }


def reference(x_words, x_scales, eT, w1, w2, w3, w4, offs):
    xq = unpack_weight(x_words, x_scales)[:, unstriped(offs)]
    h = silu(mxq(f64(w1), 0, "e4m3").T @ xq[:, :V] + mxq(f64(w2), 0, "e4m3").T @ xq[:, V:2 * V] + mxq(f64(w3), 0, "e4m3").T @ mxq(f64(eT), 0, "e4m3"))
    return mxq(f64(w4), 0, "e4m3").T @ mxq(h, 0, "e4m3")

@@ -1,0 +1,219 @@
+from contextlib import ExitStack
+
+import concourse.mybir as mybir
+from concourse.masks import make_identity
+
+K, T, S, V, H, N, J = 1024, 2048, 1024, 512, 512, 128, 512
+FLOPS = 2 * (2 * K + J) * H * V + 2 * H * N * V
+
+F32 = mybir.dt.float32
+BF16 = mybir.dt.bfloat16
+I32 = mybir.dt.int32
+U32 = mybir.dt.uint32
+U16 = mybir.dt.uint16
+U8 = mybir.dt.uint8
+FP8X4 = mybir.dt.float8_e4m3fn_x4
+SILU = mybir.ActivationFunctionType.Silu
+
+P = 128
+PACK = 4
+K_PASS = P * PACK
+X_PASSES = K // K_PASS
+EDGES = 128
+CHUNKS = V // EDGES
+
+
+def tile_picked_edgeup_silu_p_kernel(tc, x_words, x_scales, eT, w1, w2, w3, w4, offs, out):
+    nc = tc.nc
+    with ExitStack() as ctx:
+        keep = ctx.enter_context(tc.tile_pool(name="keep", bufs=1))
+        psum = ctx.enter_context(tc.psum_pool(name="psum", bufs=1))
+
+        def load_rows(name, rows):
+            raw = keep.tile([P, PACK, rows.shape[1]], F32, name=name)
+            nc.sync.dma_start(out=raw[:], in_=rows.rearrange("(p j) c -> p j c", j=PACK))
+            return raw
+
+        def cast(engine_copy, grouped, raw, c0, c1, g0):
+            engine_copy(
+                out=grouped[:, g0 : g0 + c1 - c0, :].rearrange("p (c i) j -> p c j i", i=4),
+                in_=raw[:, :, c0:c1].rearrange("p j (c i) -> p c j i", i=4),
+            )
+
+        def cast_split(grouped, raw, on_vector):
+            width = raw.shape[2]
+            if on_vector > 0:
+                cast(nc.vector.tensor_copy, grouped, raw, 0, on_vector, 0)
+            if on_vector < width:
+                cast(nc.scalar.copy, grouped, raw, on_vector, width, on_vector)
+
+        def quantize(codes, scales, grouped):
+            nc.vector.quantize_mx(out=codes.bitcast(FP8X4), scales=scales, in_=grouped.rearrange("p c j -> p (c j)"))
+
+        def operand(name, width):
+            return (
+                keep.tile([P, width], U32, name=name + "_codes", align_bytes=64),
+                keep.tile([P, width], U8, name=name + "_scales", align_bytes=64),
+            )
+
+        def grouped_tile(name, width):
+            return keep.tile([P, width, PACK], BF16, name=name + "_bf16", align_bytes=64)
+
+        raw = {("w1", 0): load_rows("w1_raw0", w1[0:K_PASS, :])}
+        offsets = keep.tile([P, S // 16], U16, name="offsets")
+        nc.sync.dma_start(offsets[:], offs)
+
+        planes = keep.tile([P, T], U8, name="planes", align_bytes=64)
+        nc.gpsimd.memset(planes[:].bitcast(I32), 0)
+        for q in range(4):
+            nc.sync.dma_start(
+                out=planes[32 * q : 32 * q + 4 * X_PASSES, :].bitcast(I32),
+                in_=x_scales[:, 4 * q : 4 * q + 4, :].bitcast(I32),
+            )
+
+        identity = keep.tile([P, P], F32, name="identity")
+        make_identity(nc, identity[:])
+        warm = keep.tile([P, 1], F32, name="warm")
+        nc.scalar.activation(out=warm[:], in_=identity[:, 0:1], func=SILU)
+
+        def load_x(z):
+            table = keep.tile([P, T], U32, name="table%d" % z, align_bytes=64)
+            nc.sync.dma_start(out=table[:].bitcast(I32), in_=x_words[z].rearrange("p c r -> p (c r)").bitcast(I32))
+            return table
+
+        tables = [load_x(0)]
+        raw["w1", 1] = load_rows("w1_raw1", w1[K_PASS:K, :])
+        tables.append(load_x(1))
+        for z in range(X_PASSES):
+            raw["w2", z] = load_rows("w2_raw%d" % z, w2[K_PASS * z : K_PASS * (z + 1), :])
+        w3_raw = [load_rows("w3_raw%d" % a, w3[:, 256 * a : 256 * (a + 1)]) for a in range(2)]
+        e_raw = [load_rows("e_raw%d" % c, eT[:, EDGES * c : EDGES * (c + 1)]) for c in range(CHUNKS)]
+        w4_raw = load_rows("w4_raw", w4)
+
+        side_cols = V // 16
+        x_planes = keep.tile([P, S], U8, name="x_planes", align_bytes=64)
+        nc.vector.tensor_copy(x_planes[:], planes[:].indirect(offsets[:]))
+        x_codes = {}
+
+        def gather(side, z):
+            picked = keep.tile([P, V], U32, name="x_codes%d%d" % (side, z), align_bytes=64)
+            nc.vector.tensor_copy(picked[:], tables[z][:].indirect(offsets[:, side * side_cols : (side + 1) * side_cols]))
+            x_codes[side, z] = picked
+
+        h_banks = [psum.tile([P, H], F32, name="h_bank%d" % c, tag="h_bank%d" % c) for c in range(CHUNKS)]
+
+        def x_pass(side, z, on_vector):
+            name = "w%d" % (side + 1)
+            grouped = grouped_tile("%s_%d" % (name, z), H)
+            cast_split(grouped, raw[name, z], on_vector)
+            codes, scales = operand("%s_%d" % (name, z), H)
+            quantize(codes[:], scales[:], grouped[:])
+            for c in range(CHUNKS):
+                nc.tensor.matmul_mx(
+                    out=h_banks[c][:],
+                    lhsT=x_codes[side, z][:, EDGES * c : EDGES * (c + 1)].bitcast(FP8X4),
+                    lhsT_scale=x_planes[4 * z :, V * side + EDGES * c : V * side + EDGES * (c + 1)],
+                    rhs=codes[:].bitcast(FP8X4),
+                    rhs_scale=scales[:],
+                    start=(side == 0 and z == 0),
+                    stop=False,
+                )
+
+        gather(0, 0)
+        x_pass(0, 0, 0)
+        gather(1, 0)
+        gather(0, 1)
+        x_pass(0, 1, 0)
+        gather(1, 1)
+        x_pass(1, 0, 192)
+        x_pass(1, 1, 320)
+
+        w3_codes, w3_scales = operand("w3", H)
+        for a in range(2):
+            grouped = grouped_tile("w3_%d" % a, 256)
+            cast_split(grouped, w3_raw[a], 160)
+            quantize(w3_codes[:, 256 * a : 256 * (a + 1)], w3_scales[:, 256 * a : 256 * (a + 1)], grouped[:])
+
+        e_grouped = [grouped_tile("e%d" % c, EDGES) for c in range(CHUNKS)]
+        e_ops = [operand("e%d" % c, EDGES) for c in range(CHUNKS)]
+        h_words = {}
+
+        def first_layer_end(c):
+            codes, scales = e_ops[c]
+            quantize(codes[:], scales[:], e_grouped[c][:])
+            nc.tensor.matmul_mx(
+                out=h_banks[c][:],
+                lhsT=codes[:].bitcast(FP8X4),
+                lhsT_scale=scales[:],
+                rhs=w3_codes[:].bitcast(FP8X4),
+                rhs_scale=w3_scales[:],
+                start=False,
+                stop=True,
+            )
+            hT = keep.tile([P, 2, P, 2], BF16, name="hT%d" % c, align_bytes=64)
+            nc.scalar.activation(out=hT[:], in_=h_banks[c][:].rearrange("v (p u e) -> v u p e", u=2, e=2), func=SILU)
+            h_words[c] = hT[:].rearrange("v u p e -> v (u p e)").bitcast(F32)
+
+        h_pairs = {}
+        h_ops = {}
+
+        def turn(c, engine_copy):
+            turned = psum.tile([P, 2, EDGES], F32, name="turned%d" % c)
+            for u in range(2):
+                nc.tensor.transpose(turned[:, u, :], h_words[c][:, P * u : P * (u + 1)], identity[:])
+            h_pairs[c] = keep.tile([P, EDGES, 2], F32, name="h_pairs%d" % c, align_bytes=64)
+            engine_copy(out=h_pairs[c][:], in_=turned[:].rearrange("p u v -> p v u"))
+
+        def quantize_h(c):
+            codes, scales = operand("h%d" % c, EDGES)
+            nc.vector.quantize_mx(
+                out=codes[:].bitcast(FP8X4), scales=scales[:], in_=h_pairs[c][:].rearrange("p v u -> p (v u)").bitcast(BF16)
+            )
+            h_ops[c] = (codes, scales)
+
+        def second_layer(acc, c):
+            codes, scales = h_ops[c]
+            nc.tensor.matmul_mx(
+                out=acc,
+                lhsT=w4_codes[:].bitcast(FP8X4),
+                lhsT_scale=w4_scales[:],
+                rhs=codes[:].bitcast(FP8X4),
+                rhs_scale=scales[:],
+                start=True,
+                stop=True,
+            )
+
+        cast_split(e_grouped[0], e_raw[0], 0)
+        cast_split(e_grouped[1], e_raw[1], 0)
+        first_layer_end(0)
+        first_layer_end(1)
+        cast_split(e_grouped[2], e_raw[2], EDGES)
+        cast_split(e_grouped[3], e_raw[3], EDGES)
+        first_layer_end(2)
+        first_layer_end(3)
+        w4_grouped = grouped_tile("w4", N)
+        cast_split(w4_grouped, w4_raw, N)
+        turn(0, nc.vector.tensor_copy)
+        w4_codes, w4_scales = operand("w4", N)
+        quantize(w4_codes[:], w4_scales[:], w4_grouped[:])
+        quantize_h(0)
+        turn(1, nc.vector.tensor_copy)
+        turn(2, nc.vector.tensor_copy)
+        quantize_h(1)
+        quantize_h(2)
+        turn(3, nc.scalar.copy)
+        quantize_h(3)
+
+        early = EDGES * (CHUNKS - 1)
+        acc_early = psum.tile([N, early], F32, name="acc_early", tag="h_bank0")
+        for c in range(CHUNKS - 1):
+            second_layer(acc_early[:, EDGES * c : EDGES * (c + 1)], c)
+        result_early = keep.tile([N, early], F32, name="result_early")
+        nc.scalar.copy(out=result_early[:], in_=acc_early[:])
+        nc.sync.dma_start(out=out[:, 0:early], in_=result_early[:])
+
+        acc_last = psum.tile([N, EDGES], F32, name="acc_last", tag="h_bank1")
+        second_layer(acc_last[:], CHUNKS - 1)
+        result_last = keep.tile([N, EDGES], F32, name="result_last")
+        nc.vector.tensor_copy(out=result_last[:], in_=acc_last[:])
+        nc.sync.dma_start(out=out[:, early:V], in_=result_last[:])

@@ -59,40 +59,39 @@ def tile_picked_edgeup_silu_p_kernel(tc, x_words, x_scales, eT, w1, w2, w3, w4, 
         def grouped_tile(name, width):
             return keep.tile([P, width, PACK], BF16, name=name + "_bf16", align_bytes=64)
 
-        raw = {("w1", 0): load_rows("w1_raw0", w1[0:K_PASS, :])}
+        def load_x(z):
+            table = keep.tile([P, T], U32, name="table%d" % z, tag="table%d" % z, align_bytes=64)
+            nc.sync.dma_start(out=table[:].bitcast(I32), in_=x_words[z].rearrange("p c r -> p (c r)").bitcast(I32))
+            return table
+
+        tables = [load_x(0)]
         offsets = keep.tile([P, S // 16], U16, name="offsets")
         nc.sync.dma_start(offsets[:], offs)
 
         planes = keep.tile([P, T], U8, name="planes", align_bytes=64)
         nc.gpsimd.memset(planes[:].bitcast(I32), 0)
         for q in range(4):
-            nc.sync.dma_start(
+            nc.gpsimd.dma_start(
                 out=planes[32 * q : 32 * q + 4 * X_PASSES, :].bitcast(I32),
                 in_=x_scales[:, 4 * q : 4 * q + 4, :].bitcast(I32),
             )
 
         identity = keep.tile([P, P], F32, name="identity")
         make_identity(nc, identity[:])
-        warm = keep.tile([P, 1], F32, name="warm")
-        nc.scalar.activation(out=warm[:], in_=identity[:, 0:1], func=SILU)
 
-        def load_x(z):
-            table = keep.tile([P, T], U32, name="table%d" % z, align_bytes=64)
-            nc.sync.dma_start(out=table[:].bitcast(I32), in_=x_words[z].rearrange("p c r -> p (c r)").bitcast(I32))
-            return table
-
-        tables = [load_x(0)]
-        raw["w1", 1] = load_rows("w1_raw1", w1[K_PASS:K, :])
         tables.append(load_x(1))
+        raw = {("w1", 0): load_rows("w1_raw0", w1[0:K_PASS, :])}
+        raw["w1", 1] = load_rows("w1_raw1", w1[K_PASS:K, :])
         for z in range(X_PASSES):
             raw["w2", z] = load_rows("w2_raw%d" % z, w2[K_PASS * z : K_PASS * (z + 1), :])
-        w3_raw = [load_rows("w3_raw%d" % a, w3[:, 256 * a : 256 * (a + 1)]) for a in range(2)]
-        e_raw = [load_rows("e_raw%d" % c, eT[:, EDGES * c : EDGES * (c + 1)]) for c in range(CHUNKS)]
+        w3_raw = [load_rows("w3_raw0", w3[:, 0:256])]
+        e_raw = [load_rows("e_raw0", eT[:, 0:EDGES])]
+        w3_raw.append(load_rows("w3_raw1", w3[:, 256:512]))
+        for c in range(1, CHUNKS):
+            e_raw.append(load_rows("e_raw%d" % c, eT[:, EDGES * c : EDGES * (c + 1)]))
         w4_raw = load_rows("w4_raw", w4)
 
         side_cols = V // 16
-        x_planes = keep.tile([P, S], U8, name="x_planes", align_bytes=64)
-        nc.vector.tensor_copy(x_planes[:], planes[:].indirect(offsets[:]))
         x_codes = {}
 
         def gather(side, z):
@@ -102,12 +101,16 @@ def tile_picked_edgeup_silu_p_kernel(tc, x_words, x_scales, eT, w1, w2, w3, w4, 
 
         h_banks = [psum.tile([P, H], F32, name="h_bank%d" % c, tag="h_bank%d" % c) for c in range(CHUNKS)]
 
-        def x_pass(side, z, on_vector):
+        def weight_pass(side, z, on_vector):
             name = "w%d" % (side + 1)
             grouped = grouped_tile("%s_%d" % (name, z), H)
             cast_split(grouped, raw[name, z], on_vector)
             codes, scales = operand("%s_%d" % (name, z), H)
             quantize(codes[:], scales[:], grouped[:])
+            return codes, scales
+
+        def x_pass(side, z, weights):
+            codes, scales = weights
             for c in range(CHUNKS):
                 nc.tensor.matmul_mx(
                     out=h_banks[c][:],
@@ -120,27 +123,33 @@ def tile_picked_edgeup_silu_p_kernel(tc, x_words, x_scales, eT, w1, w2, w3, w4, 
                 )
 
         gather(0, 0)
-        x_pass(0, 0, 0)
         gather(1, 0)
         gather(0, 1)
-        x_pass(0, 1, 0)
         gather(1, 1)
-        x_pass(1, 0, 192)
-        x_pass(1, 1, 320)
+        x_planes = keep.tile([P, S], U8, name="x_planes", tag="table1", align_bytes=64)
+        nc.vector.tensor_copy(x_planes[:], planes[:].indirect(offsets[:]))
+        x_pass(0, 0, weight_pass(0, 0, 0))
+        x_pass(0, 1, weight_pass(0, 1, 64))
+        x_pass(1, 0, weight_pass(1, 0, 128))
+        x_pass(1, 1, weight_pass(1, 1, 256))
 
         w3_codes, w3_scales = operand("w3", H)
-        for a in range(2):
-            grouped = grouped_tile("w3_%d" % a, 256)
-            cast_split(grouped, w3_raw[a], 160)
-            quantize(w3_codes[:, 256 * a : 256 * (a + 1)], w3_scales[:, 256 * a : 256 * (a + 1)], grouped[:])
-
         e_grouped = [grouped_tile("e%d" % c, EDGES) for c in range(CHUNKS)]
         e_ops = [operand("e%d" % c, EDGES) for c in range(CHUNKS)]
+
+        w3_grouped = [grouped_tile("w3_%d" % a, 256) for a in range(2)]
+
+        def quantize_w3(a):
+            quantize(w3_codes[:, 256 * a : 256 * (a + 1)], w3_scales[:, 256 * a : 256 * (a + 1)], w3_grouped[a][:])
+
+        def quantize_e(c):
+            codes, scales = e_ops[c]
+            quantize(codes[:], scales[:], e_grouped[c][:])
+
         h_words = {}
 
         def first_layer_end(c):
             codes, scales = e_ops[c]
-            quantize(codes[:], scales[:], e_grouped[c][:])
             nc.tensor.matmul_mx(
                 out=h_banks[c][:],
                 lhsT=codes[:].bitcast(FP8X4),
@@ -154,27 +163,21 @@ def tile_picked_edgeup_silu_p_kernel(tc, x_words, x_scales, eT, w1, w2, w3, w4, 
             nc.scalar.activation(out=hT[:], in_=h_banks[c][:].rearrange("v (p u e) -> v u p e", u=2, e=2), func=SILU)
             h_words[c] = hT[:].rearrange("v u p e -> v (u p e)").bitcast(F32)
 
-        h_pairs = {}
-        h_ops = {}
-
-        def turn(c, engine_copy):
+        def turn(c, engine_copy, pairs):
             turned = psum.tile([P, 2, EDGES], F32, name="turned%d" % c)
             for u in range(2):
                 nc.tensor.transpose(turned[:, u, :], h_words[c][:, P * u : P * (u + 1)], identity[:])
-            h_pairs[c] = keep.tile([P, EDGES, 2], F32, name="h_pairs%d" % c, align_bytes=64)
-            engine_copy(out=h_pairs[c][:], in_=turned[:].rearrange("p u v -> p v u"))
+            engine_copy(out=pairs, in_=turned[:].rearrange("p u v -> p v u"))
 
-        def quantize_h(c):
-            codes, scales = operand("h%d" % c, EDGES)
+        def second_layer(name, pairs, tag, engine_copy, result):
+            width = result.shape[1]
+            codes, scales = operand(name, width)
             nc.vector.quantize_mx(
-                out=codes[:].bitcast(FP8X4), scales=scales[:], in_=h_pairs[c][:].rearrange("p v u -> p (v u)").bitcast(BF16)
+                out=codes[:].bitcast(FP8X4), scales=scales[:], in_=pairs[:].rearrange("p v u -> p (v u)").bitcast(BF16)
             )
-            h_ops[c] = (codes, scales)
-
-        def second_layer(acc, c):
-            codes, scales = h_ops[c]
+            acc = psum.tile([N, width], F32, name=name + "_acc", tag=tag)
             nc.tensor.matmul_mx(
-                out=acc,
+                out=acc[:],
                 lhsT=w4_codes[:].bitcast(FP8X4),
                 lhsT_scale=w4_scales[:],
                 rhs=codes[:].bitcast(FP8X4),
@@ -182,38 +185,41 @@ def tile_picked_edgeup_silu_p_kernel(tc, x_words, x_scales, eT, w1, w2, w3, w4, 
                 start=True,
                 stop=True,
             )
+            engine_copy(out=result, in_=acc[:])
 
+        cast_split(w3_grouped[0], w3_raw[0], 128)
+        quantize_w3(0)
         cast_split(e_grouped[0], e_raw[0], 0)
-        cast_split(e_grouped[1], e_raw[1], 0)
+        quantize_e(0)
+        cast_split(w3_grouped[1], w3_raw[1], 256)
+        cast_split(e_grouped[1], e_raw[1], EDGES)
+        quantize_w3(1)
+        quantize_e(1)
         first_layer_end(0)
         first_layer_end(1)
         cast_split(e_grouped[2], e_raw[2], EDGES)
         cast_split(e_grouped[3], e_raw[3], EDGES)
+        quantize_e(2)
+        quantize_e(3)
         first_layer_end(2)
         first_layer_end(3)
         w4_grouped = grouped_tile("w4", N)
         cast_split(w4_grouped, w4_raw, N)
-        turn(0, nc.vector.tensor_copy)
+        half = V // 2
+        early_pairs = keep.tile([P, half, 2], F32, name="early_pairs", align_bytes=64)
+        turn(0, nc.vector.tensor_copy, early_pairs[:, 0:EDGES, :])
         w4_codes, w4_scales = operand("w4", N)
         quantize(w4_codes[:], w4_scales[:], w4_grouped[:])
-        quantize_h(0)
-        turn(1, nc.vector.tensor_copy)
-        turn(2, nc.vector.tensor_copy)
-        quantize_h(1)
-        quantize_h(2)
-        turn(3, nc.scalar.copy)
-        quantize_h(3)
+        turn(1, nc.vector.tensor_copy, early_pairs[:, EDGES:half, :])
+        late_pairs = {}
+        for c in (2, 3):
+            late_pairs[c] = keep.tile([P, EDGES, 2], F32, name="late_pairs%d" % c, align_bytes=64)
+            turn(c, nc.scalar.copy, late_pairs[c][:])
 
-        early = EDGES * (CHUNKS - 1)
-        acc_early = psum.tile([N, early], F32, name="acc_early", tag="h_bank0")
-        for c in range(CHUNKS - 1):
-            second_layer(acc_early[:, EDGES * c : EDGES * (c + 1)], c)
-        result_early = keep.tile([N, early], F32, name="result_early")
-        nc.scalar.copy(out=result_early[:], in_=acc_early[:])
-        nc.sync.dma_start(out=out[:, 0:early], in_=result_early[:])
-
-        acc_last = psum.tile([N, EDGES], F32, name="acc_last", tag="h_bank1")
-        second_layer(acc_last[:], CHUNKS - 1)
-        result_last = keep.tile([N, EDGES], F32, name="result_last")
-        nc.vector.tensor_copy(out=result_last[:], in_=acc_last[:])
-        nc.sync.dma_start(out=out[:, early:V], in_=result_last[:])
+        result_early = keep.tile([N, half], F32, name="result_early")
+        second_layer("h0", early_pairs, "h_bank0", nc.vector.tensor_copy, result_early[:])
+        nc.sync.dma_start(out=out[:, 0:half], in_=result_early[:])
+        for c, engine_copy in ((2, nc.scalar.copy), (3, nc.vector.tensor_copy)):
+            result = keep.tile([N, EDGES], F32, name="result%d" % c)
+            second_layer("h%d" % c, late_pairs[c], "h_bank%d" % (c - 1), engine_copy, result[:])
+            nc.sync.dma_start(out=out[:, EDGES * c : EDGES * (c + 1)], in_=result[:])

@@ -1,7 +1,6 @@
 from contextlib import ExitStack
 
 import concourse.mybir as mybir
-from concourse.masks import make_identity
 
 K, T, S, V, H, N, J = 1024, 2048, 1024, 512, 512, 128, 512
 FLOPS = 2 * (2 * K + J) * H * V + 2 * H * N * V
@@ -30,22 +29,21 @@ def tile_picked_edgeup_silu_p_kernel(tc, x_words, x_scales, eT, w1, w2, w3, w4, 
         psum = ctx.enter_context(tc.psum_pool(name="psum", bufs=1))
 
         def load_rows(name, rows):
-            raw = keep.tile([P, PACK, rows.shape[1]], F32, name=name)
+            raw = keep.tile([P, PACK, rows.shape[1]], F32, name=name, tag=name, align_bytes=64)
             nc.sync.dma_start(out=raw[:], in_=rows.rearrange("(p j) c -> p j c", j=PACK))
             return raw
 
-        def cast(engine_copy, grouped, raw, c0, c1, g0):
+        def cast(engine_copy, grouped, raw):
             engine_copy(
-                out=grouped[:, g0 : g0 + c1 - c0, :].rearrange("p (c i) j -> p c j i", i=4),
-                in_=raw[:, :, c0:c1].rearrange("p j (c i) -> p c j i", i=4),
+                out=grouped.rearrange("p (c i) j -> p c j i", i=4),
+                in_=raw.rearrange("p j (c i) -> p c j i", i=4),
             )
 
-        def cast_split(grouped, raw, on_vector):
-            width = raw.shape[2]
-            if on_vector > 0:
-                cast(nc.vector.tensor_copy, grouped, raw, 0, on_vector, 0)
-            if on_vector < width:
-                cast(nc.scalar.copy, grouped, raw, on_vector, width, on_vector)
+        def cast_dealt(engine_copy, grouped, raw, u, a0, a1):
+            engine_copy(
+                out=grouped[:].rearrange("p (u e a b) j -> p u a j b e", u=2, e=2, b=2)[:, u, a0:a1],
+                in_=raw[:].rearrange("p j (a u b e) -> p u a j b e", u=2, e=2, b=2)[:, u, a0:a1],
+            )
 
         def quantize(codes, scales, grouped):
             nc.vector.quantize_mx(out=codes.bitcast(FP8X4), scales=scales, in_=grouped.rearrange("p c j -> p (c j)"))
@@ -76,106 +74,100 @@ def tile_picked_edgeup_silu_p_kernel(tc, x_words, x_scales, eT, w1, w2, w3, w4, 
                 in_=x_scales[:, 4 * q : 4 * q + 4, :].bitcast(I32),
             )
 
-        identity = keep.tile([P, P], F32, name="identity")
-        make_identity(nc, identity[:])
-
         tables.append(load_x(1))
-        raw = {("w1", 0): load_rows("w1_raw0", w1[0:K_PASS, :])}
-        raw["w1", 1] = load_rows("w1_raw1", w1[K_PASS:K, :])
+        raw = {}
+        for side, w in enumerate((w1, w2)):
+            for z in range(X_PASSES):
+                raw[side, z] = load_rows("w%d_raw%d" % (side + 1, z), w[K_PASS * z : K_PASS * (z + 1), :])
+        w3_raw = load_rows("w3_raw", w3)
+        e_early = load_rows("e_raw01", eT[:, 0 : 2 * EDGES])
+        e_raw = [e_early[:, :, 0:EDGES], e_early[:, :, EDGES : 2 * EDGES]]
+        w4_raw = keep.tile([P, PACK, N], F32, name="w4_raw")
+        w4_rows = w4.rearrange("(a u b e) n -> u a b (e n)", u=2, e=2, b=2)
+        for u in range(2):
+            nc.sync.dma_start(out=w4_raw[:, 2 * u : 2 * u + 2, :].rearrange("p e n -> p (e n)"), in_=w4_rows[u])
+        for c in range(2, CHUNKS):
+            e_late = load_rows("e_raw%d" % c, eT[:, EDGES * c : EDGES * (c + 1)])
+            e_raw.append(e_late[:])
+
+        warm = keep.tile([P, 1], F32, name="warm")
+        nc.scalar.activation(out=warm[:], in_=raw[0, 0][:, 0, 0:1], func=SILU)
+
+        x_codes = []
         for z in range(X_PASSES):
-            raw["w2", z] = load_rows("w2_raw%d" % z, w2[K_PASS * z : K_PASS * (z + 1), :])
-        w3_raw = [load_rows("w3_raw0", w3[:, 0:256])]
-        e_raw = [load_rows("e_raw0", eT[:, 0:EDGES])]
-        w3_raw.append(load_rows("w3_raw1", w3[:, 256:512]))
-        for c in range(1, CHUNKS):
-            e_raw.append(load_rows("e_raw%d" % c, eT[:, EDGES * c : EDGES * (c + 1)]))
-        w4_raw = load_rows("w4_raw", w4)
+            picked = keep.tile([P, S], U32, name="x_codes%d" % z, align_bytes=64)
+            nc.vector.tensor_copy(picked[:], tables[z][:].indirect(offsets[:]))
+            x_codes.append(picked)
 
-        side_cols = V // 16
-        x_codes = {}
+        h_banks = [psum.tile([P, PACK, EDGES], F32, name="h_bank%d" % c) for c in range(CHUNKS)]
 
-        def gather(side, z):
-            picked = keep.tile([P, V], U32, name="x_codes%d%d" % (side, z), align_bytes=64)
-            nc.vector.tensor_copy(picked[:], tables[z][:].indirect(offsets[:, side * side_cols : (side + 1) * side_cols]))
-            x_codes[side, z] = picked
-
-        h_banks = [psum.tile([P, H], F32, name="h_bank%d" % c, tag="h_bank%d" % c) for c in range(CHUNKS)]
-
-        def weight_pass(side, z, on_vector):
-            name = "w%d" % (side + 1)
-            grouped = grouped_tile("%s_%d" % (name, z), H)
-            cast_split(grouped, raw[name, z], on_vector)
-            codes, scales = operand("%s_%d" % (name, z), H)
+        def stationary(name, rows, on_vector):
+            grouped = grouped_tile(name, H)
+            for u in range(2):
+                cut = min(max(on_vector - 64 * u, 0), 64)
+                if cut > 0:
+                    cast_dealt(nc.vector.tensor_copy, grouped, rows, u, 0, cut)
+                if cut < 64:
+                    cast_dealt(nc.scalar.copy, grouped, rows, u, cut, 64)
+            codes, scales = operand(name, H)
             quantize(codes[:], scales[:], grouped[:])
             return codes, scales
 
-        def x_pass(side, z, weights):
-            codes, scales = weights
-            for c in range(CHUNKS):
+        def first_layer_pass(c, weights, codes, scales, first, last):
+            w_codes, w_scales = weights
+            for t in range(PACK):
                 nc.tensor.matmul_mx(
-                    out=h_banks[c][:],
-                    lhsT=x_codes[side, z][:, EDGES * c : EDGES * (c + 1)].bitcast(FP8X4),
-                    lhsT_scale=x_planes[4 * z :, V * side + EDGES * c : V * side + EDGES * (c + 1)],
-                    rhs=codes[:].bitcast(FP8X4),
-                    rhs_scale=scales[:],
-                    start=(side == 0 and z == 0),
-                    stop=False,
+                    out=h_banks[c][:, t, :],
+                    lhsT=w_codes[:, P * t : P * (t + 1)].bitcast(FP8X4),
+                    lhsT_scale=w_scales[:, P * t : P * (t + 1)],
+                    rhs=codes.bitcast(FP8X4),
+                    rhs_scale=scales,
+                    start=(first and t == 0),
+                    stop=(last and t == PACK - 1),
                 )
 
-        gather(0, 0)
-        gather(1, 0)
-        gather(0, 1)
-        gather(1, 1)
-        x_planes = keep.tile([P, S], U8, name="x_planes", tag="table1", align_bytes=64)
-        nc.vector.tensor_copy(x_planes[:], planes[:].indirect(offsets[:]))
-        x_pass(0, 0, weight_pass(0, 0, 0))
-        x_pass(0, 1, weight_pass(0, 1, 64))
-        x_pass(1, 0, weight_pass(1, 0, 128))
-        x_pass(1, 1, weight_pass(1, 1, 256))
+        shares = {(0, 0): 80, (0, 1): 0, (1, 0): 64, (1, 1): 80}
+        for side in range(2):
+            for z in range(X_PASSES):
+                weights = stationary("w%d_%d" % (side + 1, z), raw[side, z], shares[side, z])
+                if side == 0 and z == 0:
+                    x_planes = keep.tile([P, S], U8, name="x_planes", tag="w1_raw0", align_bytes=64)
+                    nc.vector.tensor_copy(x_planes[:], planes[:].indirect(offsets[:]))
+                for c in range(CHUNKS):
+                    cols = slice(V * side + EDGES * c, V * side + EDGES * (c + 1))
+                    first_layer_pass(c, weights, x_codes[z][:, cols], x_planes[4 * z :, cols], side == 0 and z == 0, False)
 
-        w3_codes, w3_scales = operand("w3", H)
+        w3_weights = operand("w3", H)
+        w3_grouped = [grouped_tile("w3_%d" % u, 2 * P) for u in range(2)]
+
+        def cast_w3(engine_copy, u):
+            engine_copy(
+                out=w3_grouped[u][:].rearrange("p (e a b) j -> p a j b e", e=2, b=2),
+                in_=w3_raw[:].rearrange("p j (a u b e) -> p u a j b e", u=2, e=2, b=2)[:, u],
+            )
+
+        def quantize_w3(u):
+            cols = slice(2 * P * u, 2 * P * (u + 1))
+            quantize(w3_weights[0][:, cols], w3_weights[1][:, cols], w3_grouped[u][:])
+
         e_grouped = [grouped_tile("e%d" % c, EDGES) for c in range(CHUNKS)]
-        e_ops = [operand("e%d" % c, EDGES) for c in range(CHUNKS)]
+        h_grouped = [grouped_tile("h%d" % c, EDGES) for c in range(CHUNKS)]
 
-        w3_grouped = [grouped_tile("w3_%d" % a, 256) for a in range(2)]
-
-        def quantize_w3(a):
-            quantize(w3_codes[:, 256 * a : 256 * (a + 1)], w3_scales[:, 256 * a : 256 * (a + 1)], w3_grouped[a][:])
-
-        def quantize_e(c):
-            codes, scales = e_ops[c]
+        def close_first_layer(c):
+            codes, scales = operand("e%d" % c, EDGES)
             quantize(codes[:], scales[:], e_grouped[c][:])
+            first_layer_pass(c, w3_weights, codes[:], scales[:], False, True)
+            nc.scalar.activation(out=h_grouped[c][:], in_=h_banks[c][:].rearrange("p t v -> p v t"), func=SILU)
 
-        h_words = {}
+        h_ops = {}
 
-        def first_layer_end(c):
-            codes, scales = e_ops[c]
-            nc.tensor.matmul_mx(
-                out=h_banks[c][:],
-                lhsT=codes[:].bitcast(FP8X4),
-                lhsT_scale=scales[:],
-                rhs=w3_codes[:].bitcast(FP8X4),
-                rhs_scale=w3_scales[:],
-                start=False,
-                stop=True,
-            )
-            hT = keep.tile([P, 2, P, 2], BF16, name="hT%d" % c, align_bytes=64)
-            nc.scalar.activation(out=hT[:], in_=h_banks[c][:].rearrange("v (p u e) -> v u p e", u=2, e=2), func=SILU)
-            h_words[c] = hT[:].rearrange("v u p e -> v (u p e)").bitcast(F32)
+        def quantize_h(c):
+            h_ops[c] = operand("h%d" % c, EDGES)
+            quantize(h_ops[c][0][:], h_ops[c][1][:], h_grouped[c][:])
 
-        def turn(c, engine_copy, pairs):
-            turned = psum.tile([P, 2, EDGES], F32, name="turned%d" % c)
-            for u in range(2):
-                nc.tensor.transpose(turned[:, u, :], h_words[c][:, P * u : P * (u + 1)], identity[:])
-            engine_copy(out=pairs, in_=turned[:].rearrange("p u v -> p v u"))
-
-        def second_layer(name, pairs, tag, engine_copy, result):
-            width = result.shape[1]
-            codes, scales = operand(name, width)
-            nc.vector.quantize_mx(
-                out=codes[:].bitcast(FP8X4), scales=scales[:], in_=pairs[:].rearrange("p v u -> p (v u)").bitcast(BF16)
-            )
-            acc = psum.tile([N, width], F32, name=name + "_acc", tag=tag)
+        def second_layer(c, engine_copy, result):
+            codes, scales = h_ops[c]
+            acc = psum.tile([N, EDGES], F32, name="acc%d" % c)
             nc.tensor.matmul_mx(
                 out=acc[:],
                 lhsT=w4_codes[:].bitcast(FP8X4),
@@ -187,39 +179,25 @@ def tile_picked_edgeup_silu_p_kernel(tc, x_words, x_scales, eT, w1, w2, w3, w4, 
             )
             engine_copy(out=result, in_=acc[:])
 
-        cast_split(w3_grouped[0], w3_raw[0], 128)
+        cast_w3(nc.scalar.copy, 1)
+        cast_w3(nc.vector.tensor_copy, 0)
         quantize_w3(0)
-        cast_split(e_grouped[0], e_raw[0], 0)
-        quantize_e(0)
-        cast_split(w3_grouped[1], w3_raw[1], 256)
-        cast_split(e_grouped[1], e_raw[1], EDGES)
-        quantize_w3(1)
-        quantize_e(1)
-        first_layer_end(0)
-        first_layer_end(1)
-        cast_split(e_grouped[2], e_raw[2], EDGES)
-        cast_split(e_grouped[3], e_raw[3], EDGES)
-        quantize_e(2)
-        quantize_e(3)
-        first_layer_end(2)
-        first_layer_end(3)
+        cast(nc.vector.tensor_copy, e_grouped[0][:], e_raw[0])
+        cast(nc.scalar.copy, e_grouped[1][:], e_raw[1])
         w4_grouped = grouped_tile("w4", N)
-        cast_split(w4_grouped, w4_raw, N)
-        half = V // 2
-        early_pairs = keep.tile([P, half, 2], F32, name="early_pairs", align_bytes=64)
-        turn(0, nc.vector.tensor_copy, early_pairs[:, 0:EDGES, :])
+        cast(nc.scalar.copy, w4_grouped[:], w4_raw[:])
+        quantize_w3(1)
+        close_first_layer(0)
+        close_first_layer(1)
+        cast(nc.vector.tensor_copy, e_grouped[2][:], e_raw[2])
         w4_codes, w4_scales = operand("w4", N)
         quantize(w4_codes[:], w4_scales[:], w4_grouped[:])
-        turn(1, nc.vector.tensor_copy, early_pairs[:, EDGES:half, :])
-        late_pairs = {}
-        for c in (2, 3):
-            late_pairs[c] = keep.tile([P, EDGES, 2], F32, name="late_pairs%d" % c, align_bytes=64)
-            turn(c, nc.scalar.copy, late_pairs[c][:])
-
-        result_early = keep.tile([N, half], F32, name="result_early")
-        second_layer("h0", early_pairs, "h_bank0", nc.vector.tensor_copy, result_early[:])
-        nc.sync.dma_start(out=out[:, 0:half], in_=result_early[:])
-        for c, engine_copy in ((2, nc.scalar.copy), (3, nc.vector.tensor_copy)):
+        cast(nc.vector.tensor_copy, e_grouped[3][:], e_raw[3])
+        close_first_layer(2)
+        close_first_layer(3)
+        for c in range(CHUNKS):
+            quantize_h(c)
+        for c in range(CHUNKS):
             result = keep.tile([N, EDGES], F32, name="result%d" % c)
-            second_layer("h%d" % c, late_pairs[c], "h_bank%d" % (c - 1), engine_copy, result[:])
+            second_layer(c, nc.scalar.copy if c in (1, 2) else nc.vector.tensor_copy, result[:])
             nc.sync.dma_start(out=out[:, EDGES * c : EDGES * (c + 1)], in_=result[:])

@@ -99,7 +99,10 @@ def tile_picked_edgeup_silu_p_kernel(tc, x_words, x_scales, eT, w1, w2, w3, w4, 
             nc.vector.tensor_copy(picked[:], tables[z][:].indirect(offsets[:]))
             x_codes.append(picked)
 
-        h_banks = [psum.tile([P, PACK, EDGES], F32, name="h_bank%d" % c) for c in range(CHUNKS)]
+        x_planes = keep.tile([P, S], U8, name="x_planes", tag="table1", align_bytes=64)
+        nc.vector.tensor_copy(x_planes[:], planes[:].indirect(offsets[:]))
+
+        h_banks = [psum.tile([P, PACK, EDGES], F32, name="h_bank%d" % c, tag="h_bank%d" % c) for c in range(CHUNKS)]
 
         def stationary(name, rows, on_vector):
             grouped = grouped_tile(name, H)
@@ -126,13 +129,10 @@ def tile_picked_edgeup_silu_p_kernel(tc, x_words, x_scales, eT, w1, w2, w3, w4, 
                     stop=(last and t == PACK - 1),
                 )
 
-        shares = {(0, 0): 80, (0, 1): 0, (1, 0): 64, (1, 1): 80}
+        shares = {(0, 0): 0, (0, 1): 32, (1, 0): 64, (1, 1): 80}
         for side in range(2):
             for z in range(X_PASSES):
                 weights = stationary("w%d_%d" % (side + 1, z), raw[side, z], shares[side, z])
-                if side == 0 and z == 0:
-                    x_planes = keep.tile([P, S], U8, name="x_planes", tag="w1_raw0", align_bytes=64)
-                    nc.vector.tensor_copy(x_planes[:], planes[:].indirect(offsets[:]))
                 for c in range(CHUNKS):
                     cols = slice(V * side + EDGES * c, V * side + EDGES * (c + 1))
                     first_layer_pass(c, weights, x_codes[z][:, cols], x_planes[4 * z :, cols], side == 0 and z == 0, False)
@@ -157,7 +157,14 @@ def tile_picked_edgeup_silu_p_kernel(tc, x_words, x_scales, eT, w1, w2, w3, w4, 
             codes, scales = operand("e%d" % c, EDGES)
             quantize(codes[:], scales[:], e_grouped[c][:])
             first_layer_pass(c, w3_weights, codes[:], scales[:], False, True)
-            nc.scalar.activation(out=h_grouped[c][:], in_=h_banks[c][:].rearrange("p t v -> p v t"), func=SILU)
+            pieces = 2 if c == CHUNKS - 1 else 1
+            width = EDGES // pieces
+            for k in range(pieces):
+                nc.scalar.activation(
+                    out=h_grouped[c][:, width * k : width * (k + 1), :],
+                    in_=h_banks[c][:, :, width * k : width * (k + 1)].rearrange("p t v -> p v t"),
+                    func=SILU,
+                )
 
         h_ops = {}
 
@@ -195,9 +202,25 @@ def tile_picked_edgeup_silu_p_kernel(tc, x_words, x_scales, eT, w1, w2, w3, w4, 
         cast(nc.vector.tensor_copy, e_grouped[3][:], e_raw[3])
         close_first_layer(2)
         close_first_layer(3)
-        for c in range(CHUNKS):
+        for c in range(CHUNKS - 1):
             quantize_h(c)
-        for c in range(CHUNKS):
+        for c in range(CHUNKS - 1):
             result = keep.tile([N, EDGES], F32, name="result%d" % c)
             second_layer(c, nc.scalar.copy if c in (1, 2) else nc.vector.tensor_copy, result[:])
             nc.sync.dma_start(out=out[:, EDGES * c : EDGES * (c + 1)], in_=result[:])
+        result = keep.tile([N, EDGES], F32, name="result3")
+        for k in range(2):
+            codes, scales = operand("h3_%d" % k, 64)
+            quantize(codes[:], scales[:], h_grouped[3][:, 64 * k : 64 * (k + 1), :])
+            acc = psum.tile([N, 64], F32, name="acc3_%d" % k, tag="acc3" if k == 0 else "h_bank0")
+            nc.tensor.matmul_mx(
+                out=acc[:],
+                lhsT=w4_codes[:].bitcast(FP8X4),
+                lhsT_scale=w4_scales[:],
+                rhs=codes[:].bitcast(FP8X4),
+                rhs_scale=scales[:],
+                start=True,
+                stop=True,
+            )
+            (nc.vector.tensor_copy if k == 0 else nc.scalar.copy)(out=result[:, 64 * k : 64 * (k + 1)], in_=acc[:])
+        nc.sync.dma_start(out=out[:, EDGES * 3 : V], in_=result[:])

@@ -18,8 +18,14 @@ P = 128
 PACK = 4
 K_PASS = P * PACK
 X_PASSES = K // K_PASS
+QUADRANT = 32
 EDGES = 128
 CHUNKS = V // EDGES
+LAST = CHUNKS - 1
+HALF = EDGES // 2
+RUNS = P // 2
+
+VECTOR_RUNS = (0, 32, 64, 80)
 
 
 def tile_picked_edgeup_silu_p_kernel(tc, x_words, x_scales, eT, w1, w2, w3, w4, offs, out):
@@ -29,24 +35,17 @@ def tile_picked_edgeup_silu_p_kernel(tc, x_words, x_scales, eT, w1, w2, w3, w4, 
         psum = ctx.enter_context(tc.psum_pool(name="psum", bufs=1))
 
         def load_rows(name, rows):
-            raw = keep.tile([P, PACK, rows.shape[1]], F32, name=name, tag=name, align_bytes=64)
+            raw = keep.tile([P, PACK, rows.shape[1]], F32, name=name, align_bytes=64)
             nc.sync.dma_start(out=raw[:], in_=rows.rearrange("(p j) c -> p j c", j=PACK))
             return raw
 
-        def cast(engine_copy, grouped, raw):
-            engine_copy(
-                out=grouped.rearrange("p (c i) j -> p c j i", i=4),
-                in_=raw.rearrange("p j (c i) -> p c j i", i=4),
-            )
+        def load_table(z):
+            table = keep.tile([P, T], U32, name="table%d" % z, tag="table%d" % z, align_bytes=64)
+            nc.sync.dma_start(out=table[:].bitcast(I32), in_=x_words[z].rearrange("p c r -> p (c r)").bitcast(I32))
+            return table
 
-        def cast_dealt(engine_copy, grouped, raw, u, a0, a1):
-            engine_copy(
-                out=grouped[:].rearrange("p (u e a b) j -> p u a j b e", u=2, e=2, b=2)[:, u, a0:a1],
-                in_=raw[:].rearrange("p j (a u b e) -> p u a j b e", u=2, e=2, b=2)[:, u, a0:a1],
-            )
-
-        def quantize(codes, scales, grouped):
-            nc.vector.quantize_mx(out=codes.bitcast(FP8X4), scales=scales, in_=grouped.rearrange("p c j -> p (c j)"))
+        def rounded_tile(name, width):
+            return keep.tile([P, width, PACK], BF16, name=name + "_bf16", align_bytes=64)
 
         def operand(name, width):
             return (
@@ -54,70 +53,70 @@ def tile_picked_edgeup_silu_p_kernel(tc, x_words, x_scales, eT, w1, w2, w3, w4, 
                 keep.tile([P, width], U8, name=name + "_scales", align_bytes=64),
             )
 
-        def grouped_tile(name, width):
-            return keep.tile([P, width, PACK], BF16, name=name + "_bf16", align_bytes=64)
+        def round_plain(engine_copy, rounded, raw):
+            engine_copy(
+                out=rounded.rearrange("p (c i) j -> p c j i", i=4),
+                in_=raw.rearrange("p j (c i) -> p c j i", i=4),
+            )
 
-        def load_x(z):
-            table = keep.tile([P, T], U32, name="table%d" % z, tag="table%d" % z, align_bytes=64)
-            nc.sync.dma_start(out=table[:].bitcast(I32), in_=x_words[z].rearrange("p c r -> p (c r)").bitcast(I32))
-            return table
+        def round_dealt(engine_copy, rounded, raw, u, a0, a1):
+            engine_copy(
+                out=rounded.rearrange("p (e a b) j -> p a j b e", e=2, b=2)[:, a0:a1],
+                in_=raw.rearrange("p j (a u b e) -> p u a j b e", u=2, b=2, e=2)[:, u, a0:a1],
+            )
 
-        tables = [load_x(0)]
+        def quantize(codes, scales, rounded):
+            nc.vector.quantize_mx(out=codes.bitcast(FP8X4), scales=scales, in_=rounded.rearrange("p c j -> p (c j)"))
+
+        def u_columns(u):
+            return slice(2 * P * u, 2 * P * (u + 1))
+
+        def edge_columns(first, count):
+            return slice(first, first + count)
+
+        tables = [load_table(0)]
         offsets = keep.tile([P, S // 16], U16, name="offsets")
         nc.sync.dma_start(offsets[:], offs)
 
-        planes = keep.tile([P, T], U8, name="planes", align_bytes=64)
-        nc.gpsimd.memset(planes[:].bitcast(I32), 0)
-        for q in range(4):
+        scale_table = keep.tile([P, T], U8, name="scale_table", align_bytes=64)
+        nc.gpsimd.memset(scale_table[:].bitcast(I32), 0)
+        for q in range(P // QUADRANT):
             nc.gpsimd.dma_start(
-                out=planes[32 * q : 32 * q + 4 * X_PASSES, :].bitcast(I32),
+                out=scale_table[QUADRANT * q : QUADRANT * q + 4 * X_PASSES, :].bitcast(I32),
                 in_=x_scales[:, 4 * q : 4 * q + 4, :].bitcast(I32),
             )
 
-        tables.append(load_x(1))
-        raw = {}
-        for side, w in enumerate((w1, w2)):
-            for z in range(X_PASSES):
-                raw[side, z] = load_rows("w%d_raw%d" % (side + 1, z), w[K_PASS * z : K_PASS * (z + 1), :])
+        tables.append(load_table(1))
+        x_weights_raw = [
+            load_rows("w%d_raw%d" % (side + 1, z), w[K_PASS * z : K_PASS * (z + 1), :])
+            for side, w in enumerate((w1, w2))
+            for z in range(X_PASSES)
+        ]
         w3_raw = load_rows("w3_raw", w3)
-        e_early = load_rows("e_raw01", eT[:, 0 : 2 * EDGES])
-        e_raw = [e_early[:, :, 0:EDGES], e_early[:, :, EDGES : 2 * EDGES]]
-        w4_raw = keep.tile([P, PACK, N], F32, name="w4_raw")
-        w4_rows = w4.rearrange("(a u b e) n -> u a b (e n)", u=2, e=2, b=2)
+        e_pair = load_rows("e_raw01", eT[:, 0 : 2 * EDGES])
+        e_raw = [e_pair[:, :, 0:EDGES], e_pair[:, :, EDGES : 2 * EDGES]]
+        for c in range(2, CHUNKS):
+            e_single = load_rows("e_raw%d" % c, eT[:, edge_columns(EDGES * c, EDGES)])
+            e_raw.append(e_single[:])
+        w4_raw = keep.tile([P, PACK, N], F32, name="w4_raw", tag="w4_raw", align_bytes=64)
+        w4_rows = w4.rearrange("(a u b e) n -> u a b (e n)", u=2, b=2, e=2)
         for u in range(2):
             nc.sync.dma_start(out=w4_raw[:, 2 * u : 2 * u + 2, :].rearrange("p e n -> p (e n)"), in_=w4_rows[u])
-        for c in range(2, CHUNKS):
-            e_late = load_rows("e_raw%d" % c, eT[:, EDGES * c : EDGES * (c + 1)])
-            e_raw.append(e_late[:])
 
-        warm = keep.tile([P, 1], F32, name="warm")
-        nc.scalar.activation(out=warm[:], in_=raw[0, 0][:, 0, 0:1], func=SILU)
+        unread = keep.tile([P, 1], F32, name="unread")
+        nc.scalar.activation(out=unread[:], in_=x_weights_raw[0][:, 0, 0:1], func=SILU)
 
         x_codes = []
         for z in range(X_PASSES):
             picked = keep.tile([P, S], U32, name="x_codes%d" % z, align_bytes=64)
             nc.vector.tensor_copy(picked[:], tables[z][:].indirect(offsets[:]))
             x_codes.append(picked)
-
         x_planes = keep.tile([P, S], U8, name="x_planes", tag="table1", align_bytes=64)
-        nc.vector.tensor_copy(x_planes[:], planes[:].indirect(offsets[:]))
+        nc.vector.tensor_copy(x_planes[:], scale_table[:].indirect(offsets[:]))
 
-        h_banks = [psum.tile([P, PACK, EDGES], F32, name="h_bank%d" % c, tag="h_bank%d" % c) for c in range(CHUNKS)]
+        h_banks = [psum.tile([P, PACK, EDGES], F32, name="h_bank%d" % c) for c in range(CHUNKS)]
 
-        def stationary(name, rows, on_vector):
-            grouped = grouped_tile(name, H)
-            for u in range(2):
-                cut = min(max(on_vector - 64 * u, 0), 64)
-                if cut > 0:
-                    cast_dealt(nc.vector.tensor_copy, grouped, rows, u, 0, cut)
-                if cut < 64:
-                    cast_dealt(nc.scalar.copy, grouped, rows, u, cut, 64)
-            codes, scales = operand(name, H)
-            quantize(codes[:], scales[:], grouped[:])
-            return codes, scales
-
-        def first_layer_pass(c, weights, codes, scales, first, last):
-            w_codes, w_scales = weights
+        def first_layer_pass(c, w_codes, w_scales, codes, scales, first, last):
             for t in range(PACK):
                 nc.tensor.matmul_mx(
                     out=h_banks[c][:, t, :],
@@ -129,98 +128,85 @@ def tile_picked_edgeup_silu_p_kernel(tc, x_words, x_scales, eT, w1, w2, w3, w4, 
                     stop=(last and t == PACK - 1),
                 )
 
-        shares = {(0, 0): 0, (0, 1): 32, (1, 0): 64, (1, 1): 80}
-        for side in range(2):
-            for z in range(X_PASSES):
-                weights = stationary("w%d_%d" % (side + 1, z), raw[side, z], shares[side, z])
-                for c in range(CHUNKS):
-                    cols = slice(V * side + EDGES * c, V * side + EDGES * (c + 1))
-                    first_layer_pass(c, weights, x_codes[z][:, cols], x_planes[4 * z :, cols], side == 0 and z == 0, False)
+        for step, raw in enumerate(x_weights_raw):
+            side, z = divmod(step, X_PASSES)
+            rounded = rounded_tile("w%d_%d" % (side + 1, z), H)
+            for u in range(2):
+                cut = min(max(VECTOR_RUNS[step] - RUNS * u, 0), RUNS)
+                if cut > 0:
+                    round_dealt(nc.vector.tensor_copy, rounded[:, u_columns(u), :], raw[:], u, 0, cut)
+                if cut < RUNS:
+                    round_dealt(nc.scalar.copy, rounded[:, u_columns(u), :], raw[:], u, cut, RUNS)
+            w_codes, w_scales = operand("w%d_%d" % (side + 1, z), H)
+            quantize(w_codes[:], w_scales[:], rounded[:])
+            for c in range(CHUNKS):
+                entries = edge_columns(V * side + EDGES * c, EDGES)
+                first_layer_pass(c, w_codes, w_scales, x_codes[z][:, entries], x_planes[4 * z :, entries], step == 0, False)
 
-        w3_weights = operand("w3", H)
-        w3_grouped = [grouped_tile("w3_%d" % u, 2 * P) for u in range(2)]
+        w3_codes, w3_scales = operand("w3", H)
+        w3_rounded = [rounded_tile("w3_%d" % u, 2 * P) for u in range(2)]
+        e_rounded = [rounded_tile("e%d" % c, EDGES) for c in range(CHUNKS)]
+        h_pair = rounded_tile("h01", 2 * EDGES)
+        h_rounded = [h_pair[:, 0:EDGES, :], h_pair[:, EDGES : 2 * EDGES, :]]
+        for c in range(2, CHUNKS):
+            h_single = rounded_tile("h%d" % c, EDGES)
+            h_rounded.append(h_single[:])
 
-        def cast_w3(engine_copy, u):
-            engine_copy(
-                out=w3_grouped[u][:].rearrange("p (e a b) j -> p a j b e", e=2, b=2),
-                in_=w3_raw[:].rearrange("p j (a u b e) -> p u a j b e", u=2, e=2, b=2)[:, u],
-            )
-
-        def quantize_w3(u):
-            cols = slice(2 * P * u, 2 * P * (u + 1))
-            quantize(w3_weights[0][:, cols], w3_weights[1][:, cols], w3_grouped[u][:])
-
-        e_grouped = [grouped_tile("e%d" % c, EDGES) for c in range(CHUNKS)]
-        h_grouped = [grouped_tile("h%d" % c, EDGES) for c in range(CHUNKS)]
-
-        def close_first_layer(c):
+        def close_chunk(c, width):
             codes, scales = operand("e%d" % c, EDGES)
-            quantize(codes[:], scales[:], e_grouped[c][:])
-            first_layer_pass(c, w3_weights, codes[:], scales[:], False, True)
-            pieces = 2 if c == CHUNKS - 1 else 1
-            width = EDGES // pieces
-            for k in range(pieces):
+            quantize(codes[:], scales[:], e_rounded[c][:])
+            first_layer_pass(c, w3_codes, w3_scales, codes[:], scales[:], False, True)
+            for first in range(0, EDGES, width):
+                piece = edge_columns(first, width)
                 nc.scalar.activation(
-                    out=h_grouped[c][:, width * k : width * (k + 1), :],
-                    in_=h_banks[c][:, :, width * k : width * (k + 1)].rearrange("p t v -> p v t"),
-                    func=SILU,
+                    out=h_rounded[c][:, piece, :], in_=h_banks[c][:, :, piece].rearrange("p t v -> p v t"), func=SILU
                 )
 
-        h_ops = {}
+        round_dealt(nc.scalar.copy, w3_rounded[1][:], w3_raw[:], 1, 0, RUNS)
+        round_dealt(nc.vector.tensor_copy, w3_rounded[0][:], w3_raw[:], 0, 0, RUNS)
+        quantize(w3_codes[:, u_columns(0)], w3_scales[:, u_columns(0)], w3_rounded[0][:])
+        round_plain(nc.vector.tensor_copy, e_rounded[0][:], e_raw[0])
+        round_plain(nc.scalar.copy, e_rounded[1][:], e_raw[1])
+        quantize(w3_codes[:, u_columns(1)], w3_scales[:, u_columns(1)], w3_rounded[1][:])
+        close_chunk(0, EDGES)
+        close_chunk(1, EDGES)
+        round_plain(nc.vector.tensor_copy, e_rounded[2][:], e_raw[2])
+        close_chunk(2, EDGES)
+        round_plain(nc.vector.tensor_copy, e_rounded[LAST][:], e_raw[LAST])
+        close_chunk(LAST, HALF)
 
-        def quantize_h(c):
-            h_ops[c] = operand("h%d" % c, EDGES)
-            quantize(h_ops[c][0][:], h_ops[c][1][:], h_grouped[c][:])
+        w4_rounded = rounded_tile("w4", N)
+        round_plain(nc.vector.tensor_copy, w4_rounded[:], w4_raw[:])
+        early_codes = keep.tile([P, LAST * EDGES], U32, name="early_codes", tag="w4_raw", align_bytes=64)
+        early_scales = keep.tile([P, LAST * EDGES], U8, name="early_scales", align_bytes=64)
+        pair_edges = edge_columns(0, 2 * EDGES)
+        third_edges = edge_columns(2 * EDGES, EDGES)
+        quantize(early_codes[:, pair_edges], early_scales[:, pair_edges], h_pair[:])
+        w4_codes, w4_scales = operand("w4", N)
+        quantize(w4_codes[:], w4_scales[:], w4_rounded[:])
+        quantize(early_codes[:, third_edges], early_scales[:, third_edges], h_rounded[2])
 
-        def second_layer(c, engine_copy, result):
-            codes, scales = h_ops[c]
-            acc = psum.tile([N, EDGES], F32, name="acc%d" % c)
+        def second_layer(name, codes, scales, engine_copy, result):
+            acc = psum.tile([N, result.shape[1]], F32, name=name)
             nc.tensor.matmul_mx(
                 out=acc[:],
                 lhsT=w4_codes[:].bitcast(FP8X4),
                 lhsT_scale=w4_scales[:],
-                rhs=codes[:].bitcast(FP8X4),
-                rhs_scale=scales[:],
+                rhs=codes.bitcast(FP8X4),
+                rhs_scale=scales,
                 start=True,
                 stop=True,
             )
             engine_copy(out=result, in_=acc[:])
 
-        cast_w3(nc.scalar.copy, 1)
-        cast_w3(nc.vector.tensor_copy, 0)
-        quantize_w3(0)
-        cast(nc.vector.tensor_copy, e_grouped[0][:], e_raw[0])
-        cast(nc.scalar.copy, e_grouped[1][:], e_raw[1])
-        w4_grouped = grouped_tile("w4", N)
-        cast(nc.scalar.copy, w4_grouped[:], w4_raw[:])
-        quantize_w3(1)
-        close_first_layer(0)
-        close_first_layer(1)
-        cast(nc.vector.tensor_copy, e_grouped[2][:], e_raw[2])
-        w4_codes, w4_scales = operand("w4", N)
-        quantize(w4_codes[:], w4_scales[:], w4_grouped[:])
-        cast(nc.vector.tensor_copy, e_grouped[3][:], e_raw[3])
-        close_first_layer(2)
-        close_first_layer(3)
-        for c in range(CHUNKS - 1):
-            quantize_h(c)
-        for c in range(CHUNKS - 1):
-            result = keep.tile([N, EDGES], F32, name="result%d" % c)
-            second_layer(c, nc.scalar.copy if c in (1, 2) else nc.vector.tensor_copy, result[:])
-            nc.sync.dma_start(out=out[:, EDGES * c : EDGES * (c + 1)], in_=result[:])
-        result = keep.tile([N, EDGES], F32, name="result3")
-        for k in range(2):
-            codes, scales = operand("h3_%d" % k, 64)
-            quantize(codes[:], scales[:], h_grouped[3][:, 64 * k : 64 * (k + 1), :])
-            acc = psum.tile([N, 64], F32, name="acc3_%d" % k, tag="acc3" if k == 0 else "h_bank0")
-            nc.tensor.matmul_mx(
-                out=acc[:],
-                lhsT=w4_codes[:].bitcast(FP8X4),
-                lhsT_scale=w4_scales[:],
-                rhs=codes[:].bitcast(FP8X4),
-                rhs_scale=scales[:],
-                start=True,
-                stop=True,
-            )
-            (nc.vector.tensor_copy if k == 0 else nc.scalar.copy)(out=result[:, 64 * k : 64 * (k + 1)], in_=acc[:])
-        nc.sync.dma_start(out=out[:, EDGES * 3 : V], in_=result[:])
+        for name, edges, engine_copy in (("pair", pair_edges, nc.vector.tensor_copy), ("third", third_edges, nc.scalar.copy)):
+            result = keep.tile([N, edges.stop - edges.start], F32, name=name + "_result")
+            second_layer(name + "_acc", early_codes[:, edges], early_scales[:, edges], engine_copy, result[:])
+            nc.sync.dma_start(out=out[:, edges], in_=result[:])
+        last_result = keep.tile([N, EDGES], F32, name="last_result")
+        for k, engine_copy in enumerate((nc.vector.tensor_copy, nc.scalar.copy)):
+            piece = edge_columns(HALF * k, HALF)
+            codes, scales = operand("h_last%d" % k, HALF)
+            quantize(codes[:], scales[:], h_rounded[LAST][:, piece, :])
+            second_layer("last_acc%d" % k, codes[:], scales[:], engine_copy, last_result[:, piece])
+        nc.sync.dma_start(out=out[:, edge_columns(EDGES * LAST, EDGES)], in_=last_result[:])

@@ -35,7 +35,7 @@ def tile_picked_edgeup_silu_p_kernel(tc, x_words, x_scales, eT, w1, w2, w3, w4, 
         psum = ctx.enter_context(tc.psum_pool(name="psum", bufs=1))
 
         def load_rows(name, rows):
-            raw = keep.tile([P, PACK, rows.shape[1]], F32, name=name, align_bytes=64)
+            raw = keep.tile([P, PACK, rows.shape[1]], F32, name=name, tag=name, align_bytes=64)
             nc.sync.dma_start(out=raw[:], in_=rows.rearrange("(p j) c -> p j c", j=PACK))
             return raw
 
@@ -98,7 +98,7 @@ def tile_picked_edgeup_silu_p_kernel(tc, x_words, x_scales, eT, w1, w2, w3, w4, 
         for c in range(2, CHUNKS):
             e_single = load_rows("e_raw%d" % c, eT[:, edge_columns(EDGES * c, EDGES)])
             e_raw.append(e_single[:])
-        w4_raw = keep.tile([P, PACK, N], F32, name="w4_raw", tag="w4_raw", align_bytes=64)
+        w4_raw = keep.tile([P, PACK, N], F32, name="w4_raw", align_bytes=64)
         w4_rows = w4.rearrange("(a u b e) n -> u a b (e n)", u=2, b=2, e=2)
         for u in range(2):
             nc.sync.dma_start(out=w4_raw[:, 2 * u : 2 * u + 2, :].rearrange("p e n -> p (e n)"), in_=w4_rows[u])
@@ -148,9 +148,9 @@ def tile_picked_edgeup_silu_p_kernel(tc, x_words, x_scales, eT, w1, w2, w3, w4, 
         e_rounded = [rounded_tile("e%d" % c, EDGES) for c in range(CHUNKS)]
         h_pair = rounded_tile("h01", 2 * EDGES)
         h_rounded = [h_pair[:, 0:EDGES, :], h_pair[:, EDGES : 2 * EDGES, :]]
-        for c in range(2, CHUNKS):
-            h_single = rounded_tile("h%d" % c, EDGES)
-            h_rounded.append(h_single[:])
+        h_third = rounded_tile("h2", EDGES)
+        h_last = keep.tile([P, EDGES, PACK], BF16, name="h_last", tag="h_last", align_bytes=64)
+        h_rounded.extend([h_third[:], h_last[:]])
 
         def close_chunk(c, width):
             codes, scales = operand("e%d" % c, EDGES)
@@ -177,7 +177,7 @@ def tile_picked_edgeup_silu_p_kernel(tc, x_words, x_scales, eT, w1, w2, w3, w4, 
 
         w4_rounded = rounded_tile("w4", N)
         round_plain(nc.vector.tensor_copy, w4_rounded[:], w4_raw[:])
-        early_codes = keep.tile([P, LAST * EDGES], U32, name="early_codes", tag="w4_raw", align_bytes=64)
+        early_codes = keep.tile([P, LAST * EDGES], U32, name="early_codes", tag="e_raw%d" % LAST, align_bytes=64)
         early_scales = keep.tile([P, LAST * EDGES], U8, name="early_scales", align_bytes=64)
         pair_edges = edge_columns(0, 2 * EDGES)
         third_edges = edge_columns(2 * EDGES, EDGES)
@@ -199,14 +199,17 @@ def tile_picked_edgeup_silu_p_kernel(tc, x_words, x_scales, eT, w1, w2, w3, w4, 
             )
             engine_copy(out=result, in_=acc[:])
 
-        for name, edges, engine_copy in (("pair", pair_edges, nc.vector.tensor_copy), ("third", third_edges, nc.scalar.copy)):
-            result = keep.tile([N, edges.stop - edges.start], F32, name=name + "_result")
-            second_layer(name + "_acc", early_codes[:, edges], early_scales[:, edges], engine_copy, result[:])
-            nc.sync.dma_start(out=out[:, edges], in_=result[:])
-        last_result = keep.tile([N, EDGES], F32, name="last_result")
-        for k, engine_copy in enumerate((nc.vector.tensor_copy, nc.scalar.copy)):
-            piece = edge_columns(HALF * k, HALF)
+        last_operands = []
+        for k in range(2):
             codes, scales = operand("h_last%d" % k, HALF)
-            quantize(codes[:], scales[:], h_rounded[LAST][:, piece, :])
-            second_layer("last_acc%d" % k, codes[:], scales[:], engine_copy, last_result[:, piece])
+            quantize(codes[:], scales[:], h_rounded[LAST][:, edge_columns(HALF * k, HALF), :])
+            last_operands.append((codes, scales))
+
+        for name, edges in (("pair", pair_edges), ("third", third_edges)):
+            result = keep.tile([N, edges.stop - edges.start], F32, name=name + "_result")
+            second_layer(name + "_acc", early_codes[:, edges], early_scales[:, edges], nc.scalar.copy, result[:])
+            nc.sync.dma_start(out=out[:, edges], in_=result[:])
+        last_result = keep.tile([N, EDGES], F32, name="last_result", tag="h_last", align_bytes=64)
+        for k, (codes, scales) in enumerate(last_operands):
+            second_layer("last_acc%d" % k, codes[:], scales[:], nc.vector.tensor_copy, last_result[:, edge_columns(HALF * k, HALF)])
         nc.sync.dma_start(out=out[:, edge_columns(EDGES * LAST, EDGES)], in_=last_result[:])

@@ -25,7 +25,7 @@ LAST = CHUNKS - 1
 HALF = EDGES // 2
 RUNS = P // 2
 
-VECTOR_RUNS = (0, 32, 64, 80)
+VECTOR_RUNS = (80, 0, 64, 80)
 
 
 def tile_picked_edgeup_silu_p_kernel(tc, x_words, x_scales, eT, w1, w2, w3, w4, offs, out):
@@ -79,7 +79,7 @@ def tile_picked_edgeup_silu_p_kernel(tc, x_words, x_scales, eT, w1, w2, w3, w4, 
         nc.sync.dma_start(offsets[:], offs)
 
         scale_table = keep.tile([P, T], U8, name="scale_table", align_bytes=64)
-        nc.gpsimd.memset(scale_table[:].bitcast(I32), 0)
+        nc.vector.memset(scale_table[:].bitcast(I32), 0)
         for q in range(P // QUADRANT):
             nc.gpsimd.dma_start(
                 out=scale_table[QUADRANT * q : QUADRANT * q + 4 * X_PASSES, :].bitcast(I32),
@@ -111,8 +111,6 @@ def tile_picked_edgeup_silu_p_kernel(tc, x_words, x_scales, eT, w1, w2, w3, w4, 
             picked = keep.tile([P, S], U32, name="x_codes%d" % z, align_bytes=64)
             nc.vector.tensor_copy(picked[:], tables[z][:].indirect(offsets[:]))
             x_codes.append(picked)
-        x_planes = keep.tile([P, S], U8, name="x_planes", tag="table1", align_bytes=64)
-        nc.vector.tensor_copy(x_planes[:], scale_table[:].indirect(offsets[:]))
 
         h_banks = [psum.tile([P, PACK, EDGES], F32, name="h_bank%d" % c) for c in range(CHUNKS)]
 
@@ -139,6 +137,9 @@ def tile_picked_edgeup_silu_p_kernel(tc, x_words, x_scales, eT, w1, w2, w3, w4, 
                     round_dealt(nc.scalar.copy, rounded[:, u_columns(u), :], raw[:], u, cut, RUNS)
             w_codes, w_scales = operand("w%d_%d" % (side + 1, z), H)
             quantize(w_codes[:], w_scales[:], rounded[:])
+            if step == 0:
+                x_planes = keep.tile([P, S], U8, name="x_planes", tag="w1_0_bf16", align_bytes=64)
+                nc.vector.tensor_copy(x_planes[:], scale_table[:].indirect(offsets[:]))
             for c in range(CHUNKS):
                 entries = edge_columns(V * side + EDGES * c, EDGES)
                 first_layer_pass(c, w_codes, w_scales, x_codes[z][:, entries], x_planes[4 * z :, entries], step == 0, False)

@@ -23,6 +23,7 @@ EDGES = 128
 CHUNKS = V // EDGES
 LAST = CHUNKS - 1
 HALF = EDGES // 2
+ALIGN = 256
 RUNS = P // 2
 
 VECTOR_RUNS = (80, 0, 64, 80)
@@ -35,22 +36,22 @@ def tile_picked_edgeup_silu_p_kernel(tc, x_words, x_scales, eT, w1, w2, w3, w4, 
         psum = ctx.enter_context(tc.psum_pool(name="psum", bufs=1))
 
         def load_rows(name, rows):
-            raw = keep.tile([P, PACK, rows.shape[1]], F32, name=name, tag=name, align_bytes=64)
+            raw = keep.tile([P, PACK, rows.shape[1]], F32, name=name, tag=name, align_bytes=ALIGN)
             nc.sync.dma_start(out=raw[:], in_=rows.rearrange("(p j) c -> p j c", j=PACK))
             return raw
 
         def load_table(z):
-            table = keep.tile([P, T], U32, name="table%d" % z, tag="table%d" % z, align_bytes=64)
+            table = keep.tile([P, T], U32, name="table%d" % z, tag="table%d" % z, align_bytes=ALIGN)
             nc.sync.dma_start(out=table[:].bitcast(I32), in_=x_words[z].rearrange("p c r -> p (c r)").bitcast(I32))
             return table
 
         def rounded_tile(name, width):
-            return keep.tile([P, width, PACK], BF16, name=name + "_bf16", align_bytes=64)
+            return keep.tile([P, width, PACK], BF16, name=name + "_bf16", align_bytes=ALIGN)
 
         def operand(name, width):
             return (
-                keep.tile([P, width], U32, name=name + "_codes", align_bytes=64),
-                keep.tile([P, width], U8, name=name + "_scales", align_bytes=64),
+                keep.tile([P, width], U32, name=name + "_codes", align_bytes=ALIGN),
+                keep.tile([P, width], U8, name=name + "_scales", align_bytes=ALIGN),
             )
 
         def round_plain(engine_copy, rounded, raw):
@@ -78,7 +79,7 @@ def tile_picked_edgeup_silu_p_kernel(tc, x_words, x_scales, eT, w1, w2, w3, w4, 
         offsets = keep.tile([P, S // 16], U16, name="offsets")
         nc.sync.dma_start(offsets[:], offs)
 
-        scale_table = keep.tile([P, T], U8, name="scale_table", align_bytes=64)
+        scale_table = keep.tile([P, T], U8, name="scale_table", align_bytes=ALIGN)
         nc.vector.memset(scale_table[:].bitcast(I32), 0)
         for q in range(P // QUADRANT):
             nc.gpsimd.dma_start(
@@ -98,7 +99,7 @@ def tile_picked_edgeup_silu_p_kernel(tc, x_words, x_scales, eT, w1, w2, w3, w4, 
         for c in range(2, CHUNKS):
             e_single = load_rows("e_raw%d" % c, eT[:, edge_columns(EDGES * c, EDGES)])
             e_raw.append(e_single[:])
-        w4_raw = keep.tile([P, PACK, N], F32, name="w4_raw", align_bytes=64)
+        w4_raw = keep.tile([P, PACK, N], F32, name="w4_raw", align_bytes=ALIGN)
         w4_rows = w4.rearrange("(a u b e) n -> u a b (e n)", u=2, b=2, e=2)
         for u in range(2):
             nc.sync.dma_start(out=w4_raw[:, 2 * u : 2 * u + 2, :].rearrange("p e n -> p (e n)"), in_=w4_rows[u])
@@ -108,7 +109,7 @@ def tile_picked_edgeup_silu_p_kernel(tc, x_words, x_scales, eT, w1, w2, w3, w4, 
 
         x_codes = []
         for z in range(X_PASSES):
-            picked = keep.tile([P, S], U32, name="x_codes%d" % z, align_bytes=64)
+            picked = keep.tile([P, S], U32, name="x_codes%d" % z, align_bytes=ALIGN)
             nc.vector.tensor_copy(picked[:], tables[z][:].indirect(offsets[:]))
             x_codes.append(picked)
 
@@ -138,7 +139,7 @@ def tile_picked_edgeup_silu_p_kernel(tc, x_words, x_scales, eT, w1, w2, w3, w4, 
             w_codes, w_scales = operand("w%d_%d" % (side + 1, z), H)
             quantize(w_codes[:], w_scales[:], rounded[:])
             if step == 0:
-                x_planes = keep.tile([P, S], U8, name="x_planes", tag="w1_0_bf16", align_bytes=64)
+                x_planes = keep.tile([P, S], U8, name="x_planes", tag="w1_0_bf16", align_bytes=ALIGN)
                 nc.vector.tensor_copy(x_planes[:], scale_table[:].indirect(offsets[:]))
             for c in range(CHUNKS):
                 entries = edge_columns(V * side + EDGES * c, EDGES)
@@ -150,7 +151,7 @@ def tile_picked_edgeup_silu_p_kernel(tc, x_words, x_scales, eT, w1, w2, w3, w4, 
         h_pair = rounded_tile("h01", 2 * EDGES)
         h_rounded = [h_pair[:, 0:EDGES, :], h_pair[:, EDGES : 2 * EDGES, :]]
         h_third = rounded_tile("h2", EDGES)
-        h_last = keep.tile([P, EDGES, PACK], BF16, name="h_last", tag="h_last", align_bytes=64)
+        h_last = keep.tile([P, EDGES, PACK], BF16, name="h_last", tag="h_last", align_bytes=ALIGN)
         h_rounded.extend([h_third[:], h_last[:]])
 
         def close_chunk(c, width):
@@ -178,8 +179,8 @@ def tile_picked_edgeup_silu_p_kernel(tc, x_words, x_scales, eT, w1, w2, w3, w4, 
 
         w4_rounded = rounded_tile("w4", N)
         round_plain(nc.vector.tensor_copy, w4_rounded[:], w4_raw[:])
-        early_codes = keep.tile([P, LAST * EDGES], U32, name="early_codes", tag="e_raw%d" % LAST, align_bytes=64)
-        early_scales = keep.tile([P, LAST * EDGES], U8, name="early_scales", align_bytes=64)
+        early_codes = keep.tile([P, LAST * EDGES], U32, name="early_codes", tag="e_raw%d" % LAST, align_bytes=ALIGN)
+        early_scales = keep.tile([P, LAST * EDGES], U8, name="early_scales", align_bytes=ALIGN)
         pair_edges = edge_columns(0, 2 * EDGES)
         third_edges = edge_columns(2 * EDGES, EDGES)
         quantize(early_codes[:, pair_edges], early_scales[:, pair_edges], h_pair[:])
@@ -207,10 +208,10 @@ def tile_picked_edgeup_silu_p_kernel(tc, x_words, x_scales, eT, w1, w2, w3, w4, 
             last_operands.append((codes, scales))
 
         for name, edges in (("pair", pair_edges), ("third", third_edges)):
-            result = keep.tile([N, edges.stop - edges.start], F32, name=name + "_result")
+            result = keep.tile([N, edges.stop - edges.start], F32, name=name + "_result", align_bytes=ALIGN)
             second_layer(name + "_acc", early_codes[:, edges], early_scales[:, edges], nc.scalar.copy, result[:])
             nc.sync.dma_start(out=out[:, edges], in_=result[:])
-        last_result = keep.tile([N, EDGES], F32, name="last_result", tag="h_last", align_bytes=64)
+        last_result = keep.tile([N, EDGES], F32, name="last_result", tag="h_last", align_bytes=ALIGN)
         for k, (codes, scales) in enumerate(last_operands):
             second_layer("last_acc%d" % k, codes[:], scales[:], nc.vector.tensor_copy, last_result[:, edge_columns(HALF * k, HALF)])
         nc.sync.dma_start(out=out[:, edge_columns(EDGES * LAST, EDGES)], in_=last_result[:])

@@ -147,7 +147,10 @@ def tile_picked_edgeup_silu_p_kernel(tc, x_words, x_scales, eT, w1, w2, w3, w4, 
 
         w3_codes, w3_scales = operand("w3", H)
         w3_rounded = [rounded_tile("w3_%d" % u, 2 * P) for u in range(2)]
-        e_rounded = [rounded_tile("e%d" % c, EDGES) for c in range(CHUNKS)]
+        e_tags = ["e0_bf16", "e1_bf16", "e_raw01", "e_raw2"]
+        e_rounded = [
+            keep.tile([P, EDGES, PACK], BF16, name="e%d_bf16" % c, tag=e_tags[c], align_bytes=ALIGN) for c in range(CHUNKS)
+        ]
         h_pair = rounded_tile("h01", 2 * EDGES)
         h_rounded = [h_pair[:, 0:EDGES, :], h_pair[:, EDGES : 2 * EDGES, :]]
         h_third = rounded_tile("h2", EDGES)
@@ -156,7 +159,9 @@ def tile_picked_edgeup_silu_p_kernel(tc, x_words, x_scales, eT, w1, w2, w3, w4, 
 
         def close_chunk(c, width):
             codes, scales = operand("e%d" % c, EDGES)
-            quantize(codes[:], scales[:], e_rounded[c][:])
+            for first in range(0, EDGES, width):
+                piece = edge_columns(first, width)
+                quantize(codes[:, piece], scales[:, piece], e_rounded[c][:, piece, :])
             first_layer_pass(c, w3_codes, w3_scales, codes[:], scales[:], False, True)
             for first in range(0, EDGES, width):
                 piece = edge_columns(first, width)
@@ -174,7 +179,9 @@ def tile_picked_edgeup_silu_p_kernel(tc, x_words, x_scales, eT, w1, w2, w3, w4, 
         close_chunk(1, EDGES)
         round_plain(nc.vector.tensor_copy, e_rounded[2][:], e_raw[2])
         close_chunk(2, EDGES)
-        round_plain(nc.vector.tensor_copy, e_rounded[LAST][:], e_raw[LAST])
+        for first in range(0, EDGES, HALF):
+            piece = edge_columns(first, HALF)
+            round_plain(nc.vector.tensor_copy, e_rounded[LAST][:, piece, :], e_raw[LAST][:, :, piece])
         close_chunk(LAST, HALF)
 
         w4_rounded = rounded_tile("w4", N)

@@ -26,7 +26,7 @@ HALF = EDGES // 2
 ALIGN = 256
 RUNS = P // 2
 
-VECTOR_RUNS = (80, 0, 64, 80)
+VECTOR_RUNS = (0, 0, 64, 80)
 
 
 def tile_picked_edgeup_silu_p_kernel(tc, x_words, x_scales, eT, w1, w2, w3, w4, offs, out):
@@ -112,6 +112,8 @@ def tile_picked_edgeup_silu_p_kernel(tc, x_words, x_scales, eT, w1, w2, w3, w4, 
             picked = keep.tile([P, S], U32, name="x_codes%d" % z, align_bytes=ALIGN)
             nc.vector.tensor_copy(picked[:], tables[z][:].indirect(offsets[:]))
             x_codes.append(picked)
+        x_planes = keep.tile([P, S], U8, name="x_planes", tag="table1", align_bytes=ALIGN)
+        nc.vector.tensor_copy(x_planes[:], scale_table[:].indirect(offsets[:]))
 
         h_banks = [psum.tile([P, PACK, EDGES], F32, name="h_bank%d" % c) for c in range(CHUNKS)]
 
@@ -138,9 +140,6 @@ def tile_picked_edgeup_silu_p_kernel(tc, x_words, x_scales, eT, w1, w2, w3, w4, 
                     round_dealt(nc.scalar.copy, rounded[:, u_columns(u), :], raw[:], u, cut, RUNS)
             w_codes, w_scales = operand("w%d_%d" % (side + 1, z), H)
             quantize(w_codes[:], w_scales[:], rounded[:])
-            if step == 0:
-                x_planes = keep.tile([P, S], U8, name="x_planes", tag="w1_0_bf16", align_bytes=ALIGN)
-                nc.vector.tensor_copy(x_planes[:], scale_table[:].indirect(offsets[:]))
             for c in range(CHUNKS):
                 entries = edge_columns(V * side + EDGES * c, EDGES)
                 first_layer_pass(c, w_codes, w_scales, x_codes[z][:, entries], x_planes[4 * z :, entries], step == 0, False)

from contextlib import ExitStack

import concourse.mybir as mybir

K, T, S, V, H, N, J = 1024, 2048, 1024, 512, 512, 128, 512
FLOPS = 2 * (2 * K + J) * H * V + 2 * H * N * V

F32 = mybir.dt.float32
BF16 = mybir.dt.bfloat16
I32 = mybir.dt.int32
U32 = mybir.dt.uint32
U16 = mybir.dt.uint16
U8 = mybir.dt.uint8
FP8X4 = mybir.dt.float8_e4m3fn_x4
SILU = mybir.ActivationFunctionType.Silu

P = 128
PACK = 4
K_PASS = P * PACK
X_PASSES = K // K_PASS
QUADRANT = 32
EDGES = 128
CHUNKS = V // EDGES
LAST = CHUNKS - 1
HALF = EDGES // 2
ALIGN = 256
RUNS = P // 2

VECTOR_RUNS = (0, 0, 64, 80)


def tile_picked_edgeup_silu_p_kernel(tc, x_words, x_scales, eT, w1, w2, w3, w4, offs, out):
    nc = tc.nc
    with ExitStack() as ctx:
        keep = ctx.enter_context(tc.tile_pool(name="keep", bufs=1))
        psum = ctx.enter_context(tc.psum_pool(name="psum", bufs=1))

        def load_rows(name, rows):
            raw = keep.tile([P, PACK, rows.shape[1]], F32, name=name, tag=name, align_bytes=ALIGN)
            nc.sync.dma_start(out=raw[:], in_=rows.rearrange("(p j) c -> p j c", j=PACK))
            return raw

        def load_table(z):
            table = keep.tile([P, T], U32, name="table%d" % z, tag="table%d" % z, align_bytes=ALIGN)
            nc.sync.dma_start(out=table[:].bitcast(I32), in_=x_words[z].rearrange("p c r -> p (c r)").bitcast(I32))
            return table

        def rounded_tile(name, width):
            return keep.tile([P, width, PACK], BF16, name=name + "_bf16", align_bytes=ALIGN)

        def operand(name, width):
            return (
                keep.tile([P, width], U32, name=name + "_codes", align_bytes=ALIGN),
                keep.tile([P, width], U8, name=name + "_scales", align_bytes=ALIGN),
            )

        def round_plain(engine_copy, rounded, raw):
            engine_copy(
                out=rounded.rearrange("p (c i) j -> p c j i", i=4),
                in_=raw.rearrange("p j (c i) -> p c j i", i=4),
            )

        def round_dealt(engine_copy, rounded, raw, u, a0, a1):
            engine_copy(
                out=rounded.rearrange("p (e a b) j -> p a j b e", e=2, b=2)[:, a0:a1],
                in_=raw.rearrange("p j (a u b e) -> p u a j b e", u=2, b=2, e=2)[:, u, a0:a1],
            )

        def quantize(codes, scales, rounded):
            nc.vector.quantize_mx(out=codes.bitcast(FP8X4), scales=scales, in_=rounded.rearrange("p c j -> p (c j)"))

        def u_columns(u):
            return slice(2 * P * u, 2 * P * (u + 1))

        def edge_columns(first, count):
            return slice(first, first + count)

        tables = [load_table(0)]
        offsets = keep.tile([P, S // 16], U16, name="offsets")
        nc.sync.dma_start(offsets[:], offs)

        scale_table = keep.tile([P, T], U8, name="scale_table", align_bytes=ALIGN)
        nc.vector.memset(scale_table[:].bitcast(I32), 0)
        for q in range(P // QUADRANT):
            nc.gpsimd.dma_start(
                out=scale_table[QUADRANT * q : QUADRANT * q + 4 * X_PASSES, :].bitcast(I32),
                in_=x_scales[:, 4 * q : 4 * q + 4, :].bitcast(I32),
            )

        tables.append(load_table(1))
        x_weights_raw = [
            load_rows("w%d_raw%d" % (side + 1, z), w[K_PASS * z : K_PASS * (z + 1), :])
            for side, w in enumerate((w1, w2))
            for z in range(X_PASSES)
        ]
        w3_raw = load_rows("w3_raw", w3)
        e_pair = load_rows("e_raw01", eT[:, 0 : 2 * EDGES])
        e_raw = [e_pair[:, :, 0:EDGES], e_pair[:, :, EDGES : 2 * EDGES]]
        for c in range(2, CHUNKS):
            e_single = load_rows("e_raw%d" % c, eT[:, edge_columns(EDGES * c, EDGES)])
            e_raw.append(e_single[:])
        w4_raw = keep.tile([P, PACK, N], F32, name="w4_raw", align_bytes=ALIGN)
        w4_rows = w4.rearrange("(a u b e) n -> u a b (e n)", u=2, b=2, e=2)
        for u in range(2):
            nc.sync.dma_start(out=w4_raw[:, 2 * u : 2 * u + 2, :].rearrange("p e n -> p (e n)"), in_=w4_rows[u])

        unread = keep.tile([P, 1], F32, name="unread")
        nc.scalar.activation(out=unread[:], in_=x_weights_raw[0][:, 0, 0:1], func=SILU)

        x_codes = []
        for z in range(X_PASSES):
            picked = keep.tile([P, S], U32, name="x_codes%d" % z, align_bytes=ALIGN)
            nc.vector.tensor_copy(picked[:], tables[z][:].indirect(offsets[:]))
            x_codes.append(picked)
        x_planes = keep.tile([P, S], U8, name="x_planes", tag="table1", align_bytes=ALIGN)
        nc.vector.tensor_copy(x_planes[:], scale_table[:].indirect(offsets[:]))

        h_banks = [psum.tile([P, PACK, EDGES], F32, name="h_bank%d" % c) for c in range(CHUNKS)]

        def first_layer_pass(c, w_codes, w_scales, codes, scales, first, last):
            for t in range(PACK):
                nc.tensor.matmul_mx(
                    out=h_banks[c][:, t, :],
                    lhsT=w_codes[:, P * t : P * (t + 1)].bitcast(FP8X4),
                    lhsT_scale=w_scales[:, P * t : P * (t + 1)],
                    rhs=codes.bitcast(FP8X4),
                    rhs_scale=scales,
                    start=(first and t == 0),
                    stop=(last and t == PACK - 1),
                )

        for step, raw in enumerate(x_weights_raw):
            side, z = divmod(step, X_PASSES)
            rounded = rounded_tile("w%d_%d" % (side + 1, z), H)
            for u in range(2):
                cut = min(max(VECTOR_RUNS[step] - RUNS * u, 0), RUNS)
                if cut > 0:
                    round_dealt(nc.vector.tensor_copy, rounded[:, u_columns(u), :], raw[:], u, 0, cut)
                if cut < RUNS:
                    round_dealt(nc.scalar.copy, rounded[:, u_columns(u), :], raw[:], u, cut, RUNS)
            w_codes, w_scales = operand("w%d_%d" % (side + 1, z), H)
            quantize(w_codes[:], w_scales[:], rounded[:])
            for c in range(CHUNKS):
                entries = edge_columns(V * side + EDGES * c, EDGES)
                first_layer_pass(c, w_codes, w_scales, x_codes[z][:, entries], x_planes[4 * z :, entries], step == 0, False)

        w3_codes, w3_scales = operand("w3", H)
        w3_rounded = [rounded_tile("w3_%d" % u, 2 * P) for u in range(2)]
        e_tags = ["e0_bf16", "e1_bf16", "e_raw01", "e_raw2"]
        e_rounded = [
            keep.tile([P, EDGES, PACK], BF16, name="e%d_bf16" % c, tag=e_tags[c], align_bytes=ALIGN) for c in range(CHUNKS)
        ]
        h_pair = rounded_tile("h01", 2 * EDGES)
        h_rounded = [h_pair[:, 0:EDGES, :], h_pair[:, EDGES : 2 * EDGES, :]]
        h_third = rounded_tile("h2", EDGES)
        h_last = keep.tile([P, EDGES, PACK], BF16, name="h_last", tag="h_last", align_bytes=ALIGN)
        h_rounded.extend([h_third[:], h_last[:]])

        def close_chunk(c, width):
            codes, scales = operand("e%d" % c, EDGES)
            for first in range(0, EDGES, width):
                piece = edge_columns(first, width)
                quantize(codes[:, piece], scales[:, piece], e_rounded[c][:, piece, :])
            first_layer_pass(c, w3_codes, w3_scales, codes[:], scales[:], False, True)
            for first in range(0, EDGES, width):
                piece = edge_columns(first, width)
                nc.scalar.activation(
                    out=h_rounded[c][:, piece, :], in_=h_banks[c][:, :, piece].rearrange("p t v -> p v t"), func=SILU
                )

        round_dealt(nc.scalar.copy, w3_rounded[1][:], w3_raw[:], 1, 0, RUNS)
        round_dealt(nc.vector.tensor_copy, w3_rounded[0][:], w3_raw[:], 0, 0, RUNS)
        quantize(w3_codes[:, u_columns(0)], w3_scales[:, u_columns(0)], w3_rounded[0][:])
        round_plain(nc.vector.tensor_copy, e_rounded[0][:], e_raw[0])
        round_plain(nc.scalar.copy, e_rounded[1][:], e_raw[1])
        quantize(w3_codes[:, u_columns(1)], w3_scales[:, u_columns(1)], w3_rounded[1][:])
        close_chunk(0, EDGES)
        close_chunk(1, EDGES)
        round_plain(nc.vector.tensor_copy, e_rounded[2][:], e_raw[2])
        close_chunk(2, EDGES)
        for first in range(0, EDGES, HALF):
            piece = edge_columns(first, HALF)
            round_plain(nc.vector.tensor_copy, e_rounded[LAST][:, piece, :], e_raw[LAST][:, :, piece])
        close_chunk(LAST, HALF)

        w4_rounded = rounded_tile("w4", N)
        round_plain(nc.vector.tensor_copy, w4_rounded[:], w4_raw[:])
        early_codes = keep.tile([P, LAST * EDGES], U32, name="early_codes", tag="e_raw%d" % LAST, align_bytes=ALIGN)
        early_scales = keep.tile([P, LAST * EDGES], U8, name="early_scales", align_bytes=ALIGN)
        pair_edges = edge_columns(0, 2 * EDGES)
        third_edges = edge_columns(2 * EDGES, EDGES)
        quantize(early_codes[:, pair_edges], early_scales[:, pair_edges], h_pair[:])
        w4_codes, w4_scales = operand("w4", N)
        quantize(w4_codes[:], w4_scales[:], w4_rounded[:])
        quantize(early_codes[:, third_edges], early_scales[:, third_edges], h_rounded[2])

        def second_layer(name, codes, scales, engine_copy, result):
            acc = psum.tile([N, result.shape[1]], F32, name=name)
            nc.tensor.matmul_mx(
                out=acc[:],
                lhsT=w4_codes[:].bitcast(FP8X4),
                lhsT_scale=w4_scales[:],
                rhs=codes.bitcast(FP8X4),
                rhs_scale=scales,
                start=True,
                stop=True,
            )
            engine_copy(out=result, in_=acc[:])

        last_operands = []
        for k in range(2):
            codes, scales = operand("h_last%d" % k, HALF)
            quantize(codes[:], scales[:], h_rounded[LAST][:, edge_columns(HALF * k, HALF), :])
            last_operands.append((codes, scales))

        for name, edges in (("pair", pair_edges), ("third", third_edges)):
            result = keep.tile([N, edges.stop - edges.start], F32, name=name + "_result", align_bytes=ALIGN)
            second_layer(name + "_acc", early_codes[:, edges], early_scales[:, edges], nc.scalar.copy, result[:])
            nc.sync.dma_start(out=out[:, edges], in_=result[:])
        last_result = keep.tile([N, EDGES], F32, name="last_result", tag="h_last", align_bytes=ALIGN)
        for k, (codes, scales) in enumerate(last_operands):
            second_layer("last_acc%d" % k, codes[:], scales[:], nc.vector.tensor_copy, last_result[:, edge_columns(HALF * k, HALF)])
        nc.sync.dma_start(out=out[:, edge_columns(EDGES * LAST, EDGES)], in_=last_result[:])
